import numpy as np
import ml_dtypes


def mxq(x, axis, fmt="e4m3"):
    dtype, down = {"e4m3": (ml_dtypes.float8_e4m3fn, 7), "e5m2": (ml_dtypes.float8_e5m2, 14)}[fmt]
    v = np.moveaxis(np.asarray(x, np.float32).astype(ml_dtypes.bfloat16).astype(np.float64), axis, -1)
    blocks = v.reshape(v.shape[:-1] + (-1, 32))
    amax = np.abs(blocks).max(-1, keepdims=True)
    byte = np.maximum(np.where(amax > 0, np.frexp(amax)[1] - 1 + 127, 0) - down, 1)
    scale = np.exp2(byte - 127.0)
    codes = (blocks / scale).astype(np.float32).astype(dtype).astype(np.float64)
    return np.moveaxis((codes * scale).reshape(v.shape), -1, axis)


WIDE = False


def mx_kscale(k):
    if not WIDE:
        return np.ones(k)
    levels = np.array([10, -10, 5, -5, 0])
    if k % 512:
        return np.exp2(np.random.permutation(np.resize(levels, k // 32))).repeat(32)
    a = np.empty((k // 512, 16))
    for p in range(k // 512):
        a[p, :8] = np.random.permutation(np.resize(levels, 8))
        for g in range(8):
            far = levels[np.abs(levels - a[p, g]) >= 10]
            a[p, g + 8] = far[np.random.randint(len(far))]
    return np.exp2(a.ravel()).repeat(32)


def f64(x):
    return np.asarray(x).astype(np.float64)


def striped(idx):
    return np.tile(idx.reshape(-1, 16).T, (8, 1)).astype(np.uint16)


def unstriped(offs):
    return offs[:16].T.reshape(-1).astype(np.int64)


def pack_weight(w):
    k, n = w.shape
    w = f64(np.asarray(w, np.float32).astype(ml_dtypes.bfloat16)).reshape(k // 32, 32, n)
    amax = np.abs(w).max(1)
    byte = np.clip(np.where(amax > 0, np.frexp(amax)[1] - 1 + 127 - 7, 1), 1, 254)
    scaled = (w * np.exp2(127.0 - byte)[:, None, :]).reshape(k, n).astype(np.float32)
    words = np.ascontiguousarray(scaled.reshape(k // 512, 128, 4, n).transpose(0, 1, 3, 2)).astype(ml_dtypes.float8_e4m3fn).view(np.uint8)
    return words, np.ascontiguousarray(byte.astype(np.uint8).reshape(k // 512, 16, n))


def unpack_weight(words, scales):
    g, p, n, _ = words.shape
    vals = np.ascontiguousarray(words).view(ml_dtypes.float8_e4m3fn).astype(np.float64) * np.repeat(np.exp2(scales.astype(np.float64) - 127.0), 8, axis=1)[..., None]
    return vals.transpose(0, 1, 3, 2).reshape(g * 512, n)


E2M1 = np.array([0.0, 0.5, 1.0, 1.5, 2.0, 3.0, 4.0, 6.0, -0.0, -0.5, -1.0, -1.5, -2.0, -3.0, -4.0, -6.0])


def pack_fp4(w):
    k, n = w.shape
    w = f64(np.asarray(w, np.float32).astype(ml_dtypes.bfloat16)).reshape(k // 32, 32, n)
    amax = np.abs(w).max(1)
    mant, ex = np.frexp(amax / 6.0)
    byte = np.clip(np.where(amax > 0, np.where(mant > 0.5, ex, ex - 1) + 127, 1), 1, 254)
    scaled = (w * np.exp2(127.0 - byte)[:, None, :]).reshape(k, n).astype(np.float32)
    c = np.ascontiguousarray(scaled.reshape(k // 512, 128, 4, n).transpose(0, 1, 3, 2)).astype(ml_dtypes.float4_e2m1fn).view(np.uint8) & 0xF
    words = (c[..., 0::2] | (c[..., 1::2] << 4)).reshape(k // 512, 128, 2 * n)
    return np.ascontiguousarray(words), np.ascontiguousarray(byte.astype(np.uint8).reshape(k // 512, 16, n))


def unpack_fp4(words, scales):
    g, _, n = scales.shape
    words = np.ascontiguousarray(words).reshape(g, 128, n, 2)
    nib = np.empty((g, 128, n, 4), np.uint8)
    nib[..., 0::2] = words & 0xF
    nib[..., 1::2] = words >> 4
    vals = E2M1[nib] * np.repeat(np.exp2(scales.astype(np.float64) - 127.0), 8, axis=1)[..., None]
    return vals.transpose(0, 1, 3, 2).reshape(g * 512, n)


K, T, S, N, H = 512, 1024, 512, 128, 512


def setup_inputs():
    n = np.random.standard_normal
    s = mx_kscale(K)[:, None]
    u = mx_kscale(H)
    packed_xT = pack_weight(n((K, T)) * s)
    packed_w1 = pack_fp4(n((K, H)) / np.sqrt(K) / s)
    packed_w2 = pack_fp4(n((K, H)) / np.sqrt(K) / s)
    packed_w3 = pack_fp4(n((H, N)) / np.sqrt(H) / u[:, None])
    return {
        "x_words": packed_xT[0],
        "x_scales": packed_xT[1],
        "w1_words": packed_w1[0],
        "w1_scales": packed_w1[1],
        "w2_words": packed_w2[0],
        "w2_scales": packed_w2[1],
        "unit": (np.random.uniform(0.6, 1.4, (H, 1)) * u[:, None]).astype(np.float32),
        "w3_words": packed_w3[0],
        "w3_scales": packed_w3[1],
        "offs": striped(np.random.permutation(T)[:S]),
        "up": striped(np.random.permutation(S)),
        "dn": striped(np.random.permutation(S)),
    }


def reference(x_words, x_scales, w1_words, w1_scales, w2_words, w2_scales, unit, w3_words, w3_scales, offs, up, dn):
    xq = unpack_weight(x_words, x_scales)[:, unstriped(offs)]
    te = unpack_fp4(w2_words, w2_scales).T @ xq
    temp = np.log(np.exp(te) + 1.0) + 0.2
    cond = temp * np.sqrt(temp)
    ku = cond[:, unstriped(up)]
    tu = temp[:, unstriped(up)]
    hflux = (0.5 * (cond + ku)) * (tu - temp)
    ne = unpack_fp4(w1_words, w1_scales).T @ xq
    dens = np.log(np.exp(ne) + 1.0) + 0.2
    snd = np.sqrt(temp + 0.1)
    press = dens * temp
    pd = press[:, unstriped(dn)]
    pflux = dens * snd - (0.4 * pd)
    hid = f64(unit) * (hflux * (pflux / (np.abs(pflux) + 0.5)) + press)
    return unpack_fp4(w3_words, w3_scales).T @ mxq(hid, 0, "e4m3")

@@ -1,0 +1,245 @@
+from contextlib import ExitStack
+
+import concourse.mybir as mybir
+
+K, T, S, N, H = 512, 1024, 512, 128, 512
+FLOPS = 2 * K * H * S * 2 + 2 * H * N * S
+
+F32 = mybir.dt.float32
+BF16 = mybir.dt.bfloat16
+I32 = mybir.dt.int32
+U32 = mybir.dt.uint32
+U16 = mybir.dt.uint16
+U8 = mybir.dt.uint8
+FP8X4 = mybir.dt.float8_e4m3fn_x4
+FP4X4 = mybir.dt.float4_e2m1fn_x4
+ALU = mybir.AluOpType
+ACT = mybir.ActivationFunctionType
+
+P = 128
+PACK = 4
+SPARE = 16
+HALF = S // 2
+FLOOR = 2.0**-60
+
+
+def load_scale_rows(nc, plane, scales):
+    for q in range(4):
+        nc.sync.dma_start(
+            out=plane[32 * q : 32 * q + 4, :].bitcast(I32),
+            in_=scales[0][4 * q : 4 * q + 4, :].bitcast(I32),
+        )
+
+
+def tile_picked_yplsms_lim_p_kernel(
+    tc, x_words, x_scales, w1_words, w1_scales, w2_words, w2_scales, unit, w3_words, w3_scales, offs, up, dn, out
+):
+    nc = tc.nc
+    with ExitStack() as ctx:
+        keep = ctx.enter_context(tc.tile_pool(name="keep", bufs=1))
+        psum = ctx.enter_context(tc.psum_pool(name="psum", bufs=1))
+
+        def sb(name, shape, dtype):
+            return keep.tile(shape, dtype, name=name, align_bytes=64)
+
+        def planes(name, width=S, dtype=F32):
+            return [sb("%s%d" % (name, t), [P, width], dtype) for t in range(PACK)]
+
+        offs_sb = sb("offs_sb", [P, S // 16], U16)
+        up_sb = sb("up_sb", [P, S // 16], U16)
+        dn_sb = sb("dn_sb", [P, S // 16], U16)
+        xw = sb("xw", [P, T], U32)
+        xs = sb("xs", [P, T], U8)
+        w1w = sb("w1w", [P, 2 * H], U8)
+        w2w = sb("w2w", [P, 2 * H], U8)
+        w3w = sb("w3w", [P, 2 * N], U8)
+        w1s = sb("w1s", [P, H], U8)
+        w2s = sb("w2s", [P, H], U8)
+        w3s = sb("w3s", [P, N], U8)
+        unit_sb = sb("unit_sb", [P, PACK], F32)
+
+        for plane in (xs, w2s, w1s, w3s):
+            nc.vector.memset(plane[:].bitcast(I32), 0)
+
+        nc.sync.dma_start(out=xw[:].bitcast(I32), in_=x_words[0].rearrange("p n t -> p (n t)").bitcast(I32))
+        nc.sync.dma_start(out=offs_sb[:], in_=offs)
+        nc.sync.dma_start(out=w2w[:].bitcast(I32), in_=w2_words[0].bitcast(I32))
+        load_scale_rows(nc, xs, x_scales)
+        load_scale_rows(nc, w2s, w2_scales)
+        nc.sync.dma_start(out=w1w[:].bitcast(I32), in_=w1_words[0].bitcast(I32))
+        load_scale_rows(nc, w1s, w1_scales)
+        nc.sync.dma_start(out=up_sb[:], in_=up)
+        nc.sync.dma_start(out=dn_sb[:], in_=dn)
+        nc.sync.dma_start(out=unit_sb[:], in_=unit.rearrange("(p t) o -> p (t o)", t=PACK))
+        nc.sync.dma_start(out=w3w[:].bitcast(I32), in_=w3_words[0].bitcast(I32))
+        load_scale_rows(nc, w3s, w3_scales)
+
+        soft_t = planes("soft_t", S + SPARE)
+        cond = planes("cond", S + SPARE)
+        neg_press = planes("neg_press", S + SPARE)
+        for window in soft_t + cond + neg_press:
+            nc.gpsimd.memset(window[:, S:], 0.0)
+
+        def deal_words(name, words):
+            dealt = sb(name, [P, 2 * H], U8)
+            nc.vector.tensor_copy(
+                out=dealt[:].rearrange("p (t m b) -> p t m b", t=PACK, b=2),
+                in_=words[:].rearrange("p (m t b) -> p t m b", t=PACK, b=2),
+            )
+            return dealt
+
+        def deal_scales(name, plane):
+            dealt = sb(name, [P, H], U8)
+            nc.vector.tensor_copy(
+                out=dealt[:].rearrange("p (t m) -> p t m", t=PACK),
+                in_=plane[:].rearrange("p (m t) -> p t m", t=PACK),
+            )
+            return dealt
+
+        w2w_d = deal_words("w2w_d", w2w)
+        xw_g = sb("xw_g", [P, S], U32)
+        xs_g = sb("xs_g", [P, S], U8)
+        halves = [slice(h * HALF, (h + 1) * HALF) for h in range(2)]
+
+        def pick(h):
+            entries = offs_sb[:, h * HALF // 16 : (h + 1) * HALF // 16]
+            nc.vector.tensor_copy(out=xw_g[:, halves[h]], in_=xw[:].indirect(entries))
+            nc.vector.tensor_copy(out=xs_g[:, halves[h]], in_=xs[:].indirect(entries))
+
+        pick(0)
+        w2s_d = deal_scales("w2s_d", w2s)
+        pick(1)
+        w1w_d = deal_words("w1w_d", w1w)
+        w1s_d = deal_scales("w1s_d", w1s)
+
+        half_unit = sb("half_unit", [P, PACK], F32)
+        neg_unit = sb("neg_unit", [P, PACK], F32)
+        nc.vector.tensor_scalar(half_unit[:], unit_sb[:], 0.5, None, ALU.mult)
+        nc.vector.tensor_scalar(neg_unit[:], unit_sb[:], -1.0, None, ALU.mult)
+
+        def product(bank, words, scales, t, cols):
+            nc.tensor.matmul_mx(
+                out=bank[:, cols],
+                lhsT=words[:, 2 * P * t : 2 * P * (t + 1)].bitcast(FP4X4),
+                lhsT_scale=scales[:, P * t : P * (t + 1)],
+                rhs=xw_g[:, cols].bitcast(FP8X4),
+                rhs_scale=xs_g[:, cols],
+                start=True,
+                stop=True,
+            )
+
+        te = [psum.tile([P, S], F32, name="te%d" % t, tag="te%d" % t) for t in range(PACK)]
+        ne = [psum.tile([P, S], F32, name="ne%d" % t, tag="ne%d" % t) for t in range(PACK)]
+        sig_t, sig_d = planes("sig_t"), planes("sig_d")
+        log_t, log_d = planes("log_t"), planes("log_d")
+        soft_d = planes("soft_d")
+        for cols in halves:
+            for t in range(PACK):
+                product(te[t], w2w_d, w2s_d, t, cols)
+                nc.scalar.activation(sig_t[t][:, cols], te[t][:, cols], ACT.Sigmoid, scale=-1.0)
+        for t in range(PACK):
+            product(ne[t], w1w_d, w1s_d, t, slice(0, S))
+            nc.scalar.activation(sig_d[t][:], ne[t][:], ACT.Sigmoid, scale=-1.0)
+        for t in range(PACK):
+            nc.scalar.activation(log_t[t][:], sig_t[t][:], ACT.Ln, bias=FLOOR)
+            nc.scalar.activation(log_d[t][:], sig_d[t][:], ACT.Ln, bias=FLOOR)
+            nc.vector.scalar_tensor_tensor(soft_t[t][:, :S], log_t[t][:], -1.0, te[t][:], ALU.mult, ALU.max)
+            nc.vector.scalar_tensor_tensor(soft_d[t][:], log_d[t][:], -1.0, ne[t][:], ALU.mult, ALU.max)
+
+        neg_temp = planes("neg_temp")
+        for t in range(PACK):
+            nc.gpsimd.tensor_scalar(neg_temp[t][:], soft_t[t][:, :S], -1.0, -0.2, ALU.mult, ALU.add)
+            nc.vector.scalar_tensor_tensor(neg_press[t][:, :S], soft_d[t][:], 0.2, neg_temp[t][:], ALU.add, ALU.mult)
+
+        root, sound = planes("root"), planes("sound")
+        for t in range(PACK):
+            nc.scalar.activation(root[t][:], soft_t[t][:, :S], ACT.Sqrt, bias=0.2)
+            nc.scalar.activation(sound[t][:], soft_t[t][:, :S], ACT.Sqrt, scale=6.25, bias=1.875)
+
+        outflow, pflux = planes("outflow"), planes("pflux")
+        for t in range(PACK):
+            nc.vector.scalar_tensor_tensor(cond[t][:, :S], soft_t[t][:, :S], 0.2, root[t][:], ALU.add, ALU.mult)
+            nc.vector.scalar_tensor_tensor(outflow[t][:], soft_d[t][:], 0.2, sound[t][:], ALU.add, ALU.mult)
+            nc.vector.tensor_tensor(pflux[t][:], neg_press[t][:].indirect(dn_sb[:]), outflow[t][:], ALU.add)
+
+        cond_up, soft_up = planes("cond_up"), planes("soft_up")
+        mag, mag_sq, inv = planes("mag"), planes("mag_sq"), planes("inv")
+        slope, cond_sum, hflux = planes("slope"), planes("cond_sum"), planes("hflux")
+        carried, limited = planes("carried"), planes("limited")
+        hid = sb("hid", [P, PACK, S], BF16)
+
+        def fetch_up(t):
+            nc.scalar.activation(soft_up[t][:], soft_t[t][:].indirect(up_sb[:]), ACT.Copy)
+            nc.scalar.activation(cond_up[t][:], cond[t][:].indirect(up_sb[:]), ACT.Copy)
+
+        def limiter(t):
+            nc.scalar.activation(mag[t][:], pflux[t][:], ACT.Abs)
+            nc.scalar.activation(mag_sq[t][:], mag[t][:], ACT.Square, bias=1.25)
+            nc.scalar.activation(inv[t][:], mag_sq[t][:], ACT.Abs_reciprocal_sqrt)
+
+        def heat_a(t):
+            nc.vector.tensor_tensor(slope[t][:], soft_up[t][:], soft_t[t][:, :S], ALU.subtract)
+            nc.vector.tensor_tensor(cond_sum[t][:], cond_up[t][:], cond[t][:, :S], ALU.add)
+
+        def heat_b(t):
+            nc.vector.scalar_tensor_tensor(
+                hflux[t][:], slope[t][:], half_unit[:, t : t + 1], cond_sum[t][:], ALU.mult, ALU.mult
+            )
+
+        def heat_c(t):
+            nc.vector.tensor_tensor(carried[t][:], hflux[t][:], pflux[t][:], ALU.mult)
+
+        def limit(t, cols):
+            nc.vector.tensor_tensor(limited[t][:, cols], carried[t][:, cols], inv[t][:, cols], ALU.mult)
+
+        def finish(t, cols):
+            nc.vector.scalar_tensor_tensor(
+                hid[:, t, cols], neg_press[t][:, cols], neg_unit[:, t : t + 1], limited[t][:, cols], ALU.mult, ALU.add
+            )
+
+        whole = slice(0, S)
+        fetch_up(0)
+        heat_a(0)
+        heat_b(0)
+        heat_c(0)
+        for t in range(1, PACK):
+            fetch_up(t)
+            limiter(t - 1)
+            heat_a(t)
+            limit(t - 1, whole)
+            heat_b(t)
+            finish(t - 1, whole)
+            heat_c(t)
+        limiter(PACK - 1)
+        for cols in halves:
+            limit(PACK - 1, cols)
+        for cols in halves:
+            finish(PACK - 1, cols)
+
+        for h in range(2):
+            cols = halves[h]
+            woven = sb("woven%d" % h, [P, HALF, PACK], BF16)
+            dst = woven[:].rearrange("p (c i) t -> p c t i", i=4)
+            src = hid[:, :, cols].rearrange("p t (c i) -> p c t i", i=4)
+            if h == 1:
+                nc.vector.tensor_copy(out=dst, in_=src)
+            else:
+                nc.scalar.copy(out=dst, in_=src)
+            codes = sb("codes%d" % h, [P, HALF], U32)
+            scales = sb("scales%d" % h, [P, HALF], U8)
+            nc.vector.quantize_mx(
+                out=codes[:].bitcast(FP8X4), scales=scales[:], in_=woven[:].rearrange("p c t -> p (c t)")
+            )
+            acc = psum.tile([P, S], F32, name="acc%d" % h, tag="te%d" % h)
+            nc.tensor.matmul_mx(
+                out=acc[:, :HALF],
+                lhsT=w3w[:].bitcast(FP4X4),
+                lhsT_scale=w3s[:],
+                rhs=codes[:].bitcast(FP8X4),
+                rhs_scale=scales[:],
+                start=True,
+                stop=True,
+            )
+            result = sb("result%d" % h, [P, HALF], F32)
+            nc.scalar.copy(out=result[:], in_=acc[:, :HALF])
+            nc.sync.dma_start(out=out[:, cols], in_=result[:])

@@ -1,3 +1,4 @@
+import math
 from contextlib import ExitStack
 
 import concourse.mybir as mybir
@@ -18,14 +19,13 @@ ACT = mybir.ActivationFunctionType
 
 P = 128
 PACK = 4
-SPARE = 16
 HALF = S // 2
 FLOOR = 2.0**-60
 
 
-def load_scale_rows(nc, plane, scales):
-    for q in range(4):
-        nc.sync.dma_start(
+def load_scale_rows(queues, plane, scales):
+    for q, queue in enumerate(queues):
+        queue.dma_start(
             out=plane[32 * q : 32 * q + 4, :].bitcast(I32),
             in_=scales[0][4 * q : 4 * q + 4, :].bitcast(I32),
         )
@@ -39,8 +39,8 @@ def tile_picked_yplsms_lim_p_kernel(
         keep = ctx.enter_context(tc.tile_pool(name="keep", bufs=1))
         psum = ctx.enter_context(tc.psum_pool(name="psum", bufs=1))
 
-        def sb(name, shape, dtype):
-            return keep.tile(shape, dtype, name=name, align_bytes=64)
+        def sb(name, shape, dtype, on=None):
+            return keep.tile(shape, dtype, name=name, tag=on or name, align_bytes=64)
 
         def planes(name, width=S, dtype=F32):
             return [sb("%s%d" % (name, t), [P, width], dtype) for t in range(PACK)]
@@ -58,27 +58,23 @@ def tile_picked_yplsms_lim_p_kernel(
         w3s = sb("w3s", [P, N], U8)
         unit_sb = sb("unit_sb", [P, PACK], F32)
 
-        for plane in (xs, w2s, w1s, w3s):
+        nc.gpsimd.memset(xs[:].bitcast(I32), 0)
+        for plane in (w2s, w1s, w3s):
             nc.vector.memset(plane[:].bitcast(I32), 0)
+        on_sync = [nc.sync] * 4
 
-        nc.sync.dma_start(out=xw[:].bitcast(I32), in_=x_words[0].rearrange("p n t -> p (n t)").bitcast(I32))
         nc.sync.dma_start(out=offs_sb[:], in_=offs)
         nc.sync.dma_start(out=w2w[:].bitcast(I32), in_=w2_words[0].bitcast(I32))
-        load_scale_rows(nc, xs, x_scales)
-        load_scale_rows(nc, w2s, w2_scales)
+        nc.sync.dma_start(out=xw[:].bitcast(I32), in_=x_words[0].rearrange("p n t -> p (n t)").bitcast(I32))
+        load_scale_rows(on_sync, w2s, w2_scales)
+        load_scale_rows([nc.sync, nc.sync, nc.gpsimd, nc.gpsimd], xs, x_scales)
         nc.sync.dma_start(out=w1w[:].bitcast(I32), in_=w1_words[0].bitcast(I32))
-        load_scale_rows(nc, w1s, w1_scales)
+        load_scale_rows(on_sync, w1s, w1_scales)
         nc.sync.dma_start(out=up_sb[:], in_=up)
         nc.sync.dma_start(out=dn_sb[:], in_=dn)
         nc.sync.dma_start(out=unit_sb[:], in_=unit.rearrange("(p t) o -> p (t o)", t=PACK))
         nc.sync.dma_start(out=w3w[:].bitcast(I32), in_=w3_words[0].bitcast(I32))
-        load_scale_rows(nc, w3s, w3_scales)
-
-        soft_t = planes("soft_t", S + SPARE)
-        cond = planes("cond", S + SPARE)
-        neg_press = planes("neg_press", S + SPARE)
-        for window in soft_t + cond + neg_press:
-            nc.gpsimd.memset(window[:, S:], 0.0)
+        load_scale_rows(on_sync, w3s, w3_scales)
 
         def deal_words(name, words):
             dealt = sb(name, [P, 2 * H], U8)
@@ -88,8 +84,8 @@ def tile_picked_yplsms_lim_p_kernel(
             )
             return dealt
 
-        def deal_scales(name, plane):
-            dealt = sb(name, [P, H], U8)
+        def deal_scales(name, plane, on=None):
+            dealt = sb(name, [P, H], U8, on)
             nc.vector.tensor_copy(
                 out=dealt[:].rearrange("p (t m) -> p t m", t=PACK),
                 in_=plane[:].rearrange("p (m t) -> p t m", t=PACK),
@@ -101,20 +97,19 @@ def tile_picked_yplsms_lim_p_kernel(
         xs_g = sb("xs_g", [P, S], U8)
         halves = [slice(h * HALF, (h + 1) * HALF) for h in range(2)]
 
-        def pick(h):
-            entries = offs_sb[:, h * HALF // 16 : (h + 1) * HALF // 16]
-            nc.vector.tensor_copy(out=xw_g[:, halves[h]], in_=xw[:].indirect(entries))
-            nc.vector.tensor_copy(out=xs_g[:, halves[h]], in_=xs[:].indirect(entries))
+        def entries(offsets, cols):
+            return offsets[:, cols.start // 16 : cols.stop // 16]
 
-        pick(0)
-        w2s_d = deal_scales("w2s_d", w2s)
-        pick(1)
+        nc.vector.tensor_copy(out=xw_g[:], in_=xw[:].indirect(offs_sb[:]))
+        w2s_d = deal_scales("w2s_d", w2s, on="xw")
+        for cols in halves:
+            nc.vector.tensor_copy(out=xs_g[:, cols], in_=xs[:].indirect(entries(offs_sb, cols)))
         w1w_d = deal_words("w1w_d", w1w)
         w1s_d = deal_scales("w1s_d", w1s)
 
         half_unit = sb("half_unit", [P, PACK], F32)
         neg_unit = sb("neg_unit", [P, PACK], F32)
-        nc.vector.tensor_scalar(half_unit[:], unit_sb[:], 0.5, None, ALU.mult)
+        nc.vector.tensor_scalar(half_unit[:], unit_sb[:], -0.5, None, ALU.mult)
         nc.vector.tensor_scalar(neg_unit[:], unit_sb[:], -1.0, None, ALU.mult)
 
         def product(bank, words, scales, t, cols):
@@ -131,108 +126,103 @@ def tile_picked_yplsms_lim_p_kernel(
         te = [psum.tile([P, S], F32, name="te%d" % t, tag="te%d" % t) for t in range(PACK)]
         ne = [psum.tile([P, S], F32, name="ne%d" % t, tag="ne%d" % t) for t in range(PACK)]
         sig_t, sig_d = planes("sig_t"), planes("sig_d")
-        log_t, log_d = planes("log_t"), planes("log_d")
-        soft_d = planes("soft_d")
+
+        def rows(name, on=None):
+            return sb(name, [P, PACK, S], F32, on)
+
+        soft_d, neg_temp, cond = rows("soft_d"), rows("neg_temp"), rows("cond")
+        neg_press = planes("neg_press")
         for cols in halves:
             for t in range(PACK):
                 product(te[t], w2w_d, w2s_d, t, cols)
                 nc.scalar.activation(sig_t[t][:, cols], te[t][:, cols], ACT.Sigmoid, scale=-1.0)
+        neg_line = rows("neg_line", on="w1s")
+        for t in range(PACK):
+            nc.vector.tensor_scalar(neg_line[:, t, :], te[t][:], -1.0, -0.2, ALU.mult, ALU.add)
         for t in range(PACK):
             product(ne[t], w1w_d, w1s_d, t, slice(0, S))
             nc.scalar.activation(sig_d[t][:], ne[t][:], ACT.Sigmoid, scale=-1.0)
+        log_t, log_d = rows("log_t", on="w1w_d"), rows("log_d")
         for t in range(PACK):
-            nc.scalar.activation(log_t[t][:], sig_t[t][:], ACT.Ln, bias=FLOOR)
-            nc.scalar.activation(log_d[t][:], sig_d[t][:], ACT.Ln, bias=FLOOR)
-            nc.vector.scalar_tensor_tensor(soft_t[t][:, :S], log_t[t][:], -1.0, te[t][:], ALU.mult, ALU.max)
-            nc.vector.scalar_tensor_tensor(soft_d[t][:], log_d[t][:], -1.0, ne[t][:], ALU.mult, ALU.max)
-
-        neg_temp = planes("neg_temp")
+            nc.scalar.activation(log_t[:, t, :], sig_t[t][:], ACT.Ln, scale=math.exp(-0.2), bias=FLOOR)
+            nc.scalar.activation(log_d[:, t, :], sig_d[t][:], ACT.Ln, bias=FLOOR)
+            nc.vector.tensor_tensor(neg_temp[:, t, :], log_t[:, t, :], neg_line[:, t, :], ALU.min)
+            nc.vector.scalar_tensor_tensor(soft_d[:, t, :], log_d[:, t, :], -1.0, ne[t][:], ALU.mult, ALU.max)
         for t in range(PACK):
-            nc.gpsimd.tensor_scalar(neg_temp[t][:], soft_t[t][:, :S], -1.0, -0.2, ALU.mult, ALU.add)
-            nc.vector.scalar_tensor_tensor(neg_press[t][:, :S], soft_d[t][:], 0.2, neg_temp[t][:], ALU.add, ALU.mult)
+            nc.vector.scalar_tensor_tensor(neg_press[t][:], soft_d[:, t, :], 0.2, neg_temp[:, t, :], ALU.add, ALU.mult)
 
-        root, sound = planes("root"), planes("sound")
-        for t in range(PACK):
-            nc.scalar.activation(root[t][:], soft_t[t][:, :S], ACT.Sqrt, bias=0.2)
-            nc.scalar.activation(sound[t][:], soft_t[t][:, :S], ACT.Sqrt, scale=6.25, bias=1.875)
-
-        outflow, pflux = planes("outflow"), planes("pflux")
-        for t in range(PACK):
-            nc.vector.scalar_tensor_tensor(cond[t][:, :S], soft_t[t][:, :S], 0.2, root[t][:], ALU.add, ALU.mult)
-            nc.vector.scalar_tensor_tensor(outflow[t][:], soft_d[t][:], 0.2, sound[t][:], ALU.add, ALU.mult)
-            nc.vector.tensor_tensor(pflux[t][:], neg_press[t][:].indirect(dn_sb[:]), outflow[t][:], ALU.add)
-
-        cond_up, soft_up = planes("cond_up"), planes("soft_up")
-        mag, mag_sq, inv = planes("mag"), planes("mag_sq"), planes("inv")
-        slope, cond_sum, hflux = planes("slope"), planes("cond_sum"), planes("hflux")
-        carried, limited = planes("carried"), planes("limited")
-        hid = sb("hid", [P, PACK, S], BF16)
-
-        def fetch_up(t):
-            nc.scalar.activation(soft_up[t][:], soft_t[t][:].indirect(up_sb[:]), ACT.Copy)
-            nc.scalar.activation(cond_up[t][:], cond[t][:].indirect(up_sb[:]), ACT.Copy)
-
-        def limiter(t):
-            nc.scalar.activation(mag[t][:], pflux[t][:], ACT.Abs)
-            nc.scalar.activation(mag_sq[t][:], mag[t][:], ACT.Square, bias=1.25)
-            nc.scalar.activation(inv[t][:], mag_sq[t][:], ACT.Abs_reciprocal_sqrt)
-
-        def heat_a(t):
-            nc.vector.tensor_tensor(slope[t][:], soft_up[t][:], soft_t[t][:, :S], ALU.subtract)
-            nc.vector.tensor_tensor(cond_sum[t][:], cond_up[t][:], cond[t][:, :S], ALU.add)
-
-        def heat_b(t):
+        root, sound, outflow = rows("root"), rows("sound"), rows("outflow")
+        for pair in (slice(0, 2), slice(2, 4)):
+            nc.scalar.activation(root[:, pair, :], neg_temp[:, pair, :], ACT.Sqrt, scale=-1.0)
+            nc.scalar.activation(sound[:, pair, :], neg_temp[:, pair, :], ACT.Sqrt, scale=-6.25, bias=0.625)
+            for t in range(pair.start, pair.stop):
+                nc.vector.scalar_tensor_tensor(
+                    cond[:, t, :], neg_temp[:, t, :], half_unit[:, t : t + 1], root[:, t, :], ALU.mult, ALU.mult
+                )
             nc.vector.scalar_tensor_tensor(
-                hflux[t][:], slope[t][:], half_unit[:, t : t + 1], cond_sum[t][:], ALU.mult, ALU.mult
+                outflow[:, pair, :], soft_d[:, pair, :], 0.2, sound[:, pair, :], ALU.add, ALU.mult
             )
 
-        def heat_c(t):
-            nc.vector.tensor_tensor(carried[t][:], hflux[t][:], pflux[t][:], ALU.mult)
+        pflux, press_unit = rows("pflux"), rows("press_unit")
 
-        def limit(t, cols):
-            nc.vector.tensor_tensor(limited[t][:, cols], carried[t][:, cols], inv[t][:, cols], ALU.mult)
+        def particles(cols):
+            for t in range(PACK):
+                nc.vector.tensor_tensor(
+                    pflux[:, t, cols], neg_press[t][:].indirect(entries(dn_sb, cols)), outflow[:, t, cols], ALU.add
+                )
 
-        def finish(t, cols):
-            nc.vector.scalar_tensor_tensor(
-                hid[:, t, cols], neg_press[t][:, cols], neg_unit[:, t : t + 1], limited[t][:, cols], ALU.mult, ALU.add
+        cond_up, neg_temp_up = rows("cond_up"), rows("neg_temp_up")
+        mag, mag_sq, inv = rows("mag"), rows("mag_sq"), rows("inv")
+        slope, cond_sum, hflux = rows("slope"), rows("cond_sum"), rows("hflux")
+        carried, limited = rows("carried"), rows("limited")
+
+        def fetch_up(cols):
+            for window, fetched in ((neg_temp, neg_temp_up), (cond, cond_up)):
+                for t in range(PACK):
+                    nc.scalar.activation(fetched[:, t, cols], window[:, t, :].indirect(entries(up_sb, cols)), ACT.Copy)
+
+        def magnitude(cols):
+            nc.scalar.activation(mag[:, :, cols], pflux[:, :, cols], ACT.Abs)
+
+        def square(cols):
+            nc.scalar.activation(mag_sq[:, :, cols], mag[:, :, cols], ACT.Square, bias=1.25)
+
+        def inverse(cols):
+            nc.scalar.activation(inv[:, :, cols], mag_sq[:, :, cols], ACT.Abs_reciprocal_sqrt)
+
+        def neighbours(cols):
+            nc.vector.tensor_tensor(slope[:, :, cols], neg_temp[:, :, cols], neg_temp_up[:, :, cols], ALU.subtract)
+            nc.vector.tensor_tensor(cond_sum[:, :, cols], cond_up[:, :, cols], cond[:, :, cols], ALU.add)
+
+        def heat(cols):
+            nc.vector.tensor_tensor(hflux[:, :, cols], slope[:, :, cols], cond_sum[:, :, cols], ALU.mult)
+
+        def carry(cols):
+            nc.vector.tensor_tensor(carried[:, :, cols], hflux[:, :, cols], pflux[:, :, cols], ALU.mult)
+
+        def limit(cols):
+            nc.vector.tensor_tensor(limited[:, :, cols], carried[:, :, cols], inv[:, :, cols], ALU.mult)
+
+        def weave(cols):
+            hid = sb("hid%d" % cols.start, [P, cols.stop - cols.start, PACK], BF16)
+            nc.vector.tensor_tensor(
+                hid[:].rearrange("p (c i) t -> p c t i", i=4),
+                limited[:, :, cols].rearrange("p t (c i) -> p c t i", i=4),
+                press_unit[:, :, cols].rearrange("p t (c i) -> p c t i", i=4),
+                ALU.add,
             )
+            return hid
 
-        whole = slice(0, S)
-        fetch_up(0)
-        heat_a(0)
-        heat_b(0)
-        heat_c(0)
-        for t in range(1, PACK):
-            fetch_up(t)
-            limiter(t - 1)
-            heat_a(t)
-            limit(t - 1, whole)
-            heat_b(t)
-            finish(t - 1, whole)
-            heat_c(t)
-        limiter(PACK - 1)
-        for cols in halves:
-            limit(PACK - 1, cols)
-        for cols in halves:
-            finish(PACK - 1, cols)
-
-        for h in range(2):
-            cols = halves[h]
-            woven = sb("woven%d" % h, [P, HALF, PACK], BF16)
-            dst = woven[:].rearrange("p (c i) t -> p c t i", i=4)
-            src = hid[:, :, cols].rearrange("p t (c i) -> p c t i", i=4)
-            if h == 1:
-                nc.vector.tensor_copy(out=dst, in_=src)
-            else:
-                nc.scalar.copy(out=dst, in_=src)
-            codes = sb("codes%d" % h, [P, HALF], U32)
-            scales = sb("scales%d" % h, [P, HALF], U8)
+        def diagnose(cols, hid, bank):
+            width = cols.stop - cols.start
+            codes = sb("codes%d" % bank, [P, width], U32)
+            scales = sb("scales%d" % bank, [P, width], U8)
             nc.vector.quantize_mx(
-                out=codes[:].bitcast(FP8X4), scales=scales[:], in_=woven[:].rearrange("p c t -> p (c t)")
+                out=codes[:].bitcast(FP8X4), scales=scales[:], in_=hid[:].rearrange("p c t -> p (c t)")
             )
-            acc = psum.tile([P, S], F32, name="acc%d" % h, tag="te%d" % h)
+            acc = psum.tile([P, S], F32, name="acc%d" % bank, tag="te%d" % bank)
             nc.tensor.matmul_mx(
-                out=acc[:, :HALF],
+                out=acc[:, :width],
                 lhsT=w3w[:].bitcast(FP4X4),
                 lhsT_scale=w3s[:],
                 rhs=codes[:].bitcast(FP8X4),
@@ -240,6 +230,36 @@ def tile_picked_yplsms_lim_p_kernel(
                 start=True,
                 stop=True,
             )
-            result = sb("result%d" % h, [P, HALF], F32)
-            nc.scalar.copy(out=result[:], in_=acc[:, :HALF])
-            nc.sync.dma_start(out=out[:, cols], in_=result[:])
+            result = sb("result%d" % bank, [P, width], F32)
+            nc.scalar.copy(out=result[:], in_=acc[:, :width])
+            nc.scalar.dma_start(out=out[:, cols], in_=result[:])
+
+        first, second = halves
+        quarters = [slice(HALF, HALF + P), slice(HALF + P, S)]
+        particles(first)
+        for t in range(2):
+            nc.vector.tensor_scalar(press_unit[:, t, :], neg_press[t][:], neg_unit[:, t : t + 1], None, ALU.mult)
+        fetch_up(first)
+        magnitude(first)
+        square(first)
+        inverse(first)
+        for t in range(2, PACK):
+            nc.scalar.activation(press_unit[:, t, :], neg_press[t][:], ACT.Copy, scale=neg_unit[:, t : t + 1])
+        neighbours(first)
+        heat(first)
+        carry(first)
+        limit(first)
+        hid_first = weave(first)
+        particles(second)
+        fetch_up(second)
+        for step in (magnitude, square, inverse):
+            for cols in quarters:
+                step(cols)
+        neighbours(second)
+        diagnose(first, hid_first, 0)
+        for step in (heat, carry, limit):
+            for cols in quarters:
+                step(cols)
+        hids = [weave(cols) for cols in quarters]
+        for bank, cols in enumerate(quarters):
+            diagnose(cols, hids[bank], 1 + bank)

import math
from contextlib import ExitStack

import concourse.mybir as mybir

K, T, S, N, H = 512, 1024, 512, 128, 512
FLOPS = 2 * K * H * S * 2 + 2 * H * N * S

F32 = mybir.dt.float32
BF16 = mybir.dt.bfloat16
I32 = mybir.dt.int32
U32 = mybir.dt.uint32
U16 = mybir.dt.uint16
U8 = mybir.dt.uint8
FP8X4 = mybir.dt.float8_e4m3fn_x4
FP4X4 = mybir.dt.float4_e2m1fn_x4
ALU = mybir.AluOpType
ACT = mybir.ActivationFunctionType

P = 128
PACK = 4
HALF = S // 2
FLOOR = 2.0**-60


def load_scale_rows(queues, plane, scales):
    for q, queue in enumerate(queues):
        queue.dma_start(
            out=plane[32 * q : 32 * q + 4, :].bitcast(I32),
            in_=scales[0][4 * q : 4 * q + 4, :].bitcast(I32),
        )


def tile_picked_yplsms_lim_p_kernel(
    tc, x_words, x_scales, w1_words, w1_scales, w2_words, w2_scales, unit, w3_words, w3_scales, offs, up, dn, out
):
    nc = tc.nc
    with ExitStack() as ctx:
        keep = ctx.enter_context(tc.tile_pool(name="keep", bufs=1))
        psum = ctx.enter_context(tc.psum_pool(name="psum", bufs=1))

        def sb(name, shape, dtype, on=None):
            return keep.tile(shape, dtype, name=name, tag=on or name, align_bytes=64)

        def planes(name, width=S, dtype=F32):
            return [sb("%s%d" % (name, t), [P, width], dtype) for t in range(PACK)]

        offs_sb = sb("offs_sb", [P, S // 16], U16)
        up_sb = sb("up_sb", [P, S // 16], U16)
        dn_sb = sb("dn_sb", [P, S // 16], U16)
        xw = sb("xw", [P, T], U32)
        xs = sb("xs", [P, T], U8)
        w1w = sb("w1w", [P, 2 * H], U8)
        w2w = sb("w2w", [P, 2 * H], U8)
        w3w = sb("w3w", [P, 2 * N], U8)
        w1s = sb("w1s", [P, H], U8)
        w2s = sb("w2s", [P, H], U8)
        w3s = sb("w3s", [P, N], U8)
        unit_sb = sb("unit_sb", [P, PACK], F32)

        nc.gpsimd.memset(xs[:].bitcast(I32), 0)
        for plane in (w2s, w1s, w3s):
            nc.vector.memset(plane[:].bitcast(I32), 0)
        on_sync = [nc.sync] * 4

        nc.sync.dma_start(out=offs_sb[:], in_=offs)
        nc.sync.dma_start(out=w2w[:].bitcast(I32), in_=w2_words[0].bitcast(I32))
        nc.sync.dma_start(out=xw[:].bitcast(I32), in_=x_words[0].rearrange("p n t -> p (n t)").bitcast(I32))
        load_scale_rows(on_sync, w2s, w2_scales)
        load_scale_rows([nc.sync, nc.sync, nc.gpsimd, nc.gpsimd], xs, x_scales)
        nc.sync.dma_start(out=w1w[:].bitcast(I32), in_=w1_words[0].bitcast(I32))
        load_scale_rows(on_sync, w1s, w1_scales)
        nc.sync.dma_start(out=up_sb[:], in_=up)
        nc.sync.dma_start(out=dn_sb[:], in_=dn)
        nc.sync.dma_start(out=unit_sb[:], in_=unit.rearrange("(p t) o -> p (t o)", t=PACK))
        nc.sync.dma_start(out=w3w[:].bitcast(I32), in_=w3_words[0].bitcast(I32))
        load_scale_rows(on_sync, w3s, w3_scales)

        def deal_words(name, words):
            dealt = sb(name, [P, 2 * H], U8)
            nc.vector.tensor_copy(
                out=dealt[:].rearrange("p (t m b) -> p t m b", t=PACK, b=2),
                in_=words[:].rearrange("p (m t b) -> p t m b", t=PACK, b=2),
            )
            return dealt

        def deal_scales(name, plane, on=None):
            dealt = sb(name, [P, H], U8, on)
            nc.vector.tensor_copy(
                out=dealt[:].rearrange("p (t m) -> p t m", t=PACK),
                in_=plane[:].rearrange("p (m t) -> p t m", t=PACK),
            )
            return dealt

        w2w_d = deal_words("w2w_d", w2w)
        xw_g = sb("xw_g", [P, S], U32)
        xs_g = sb("xs_g", [P, S], U8)
        halves = [slice(h * HALF, (h + 1) * HALF) for h in range(2)]

        def entries(offsets, cols):
            return offsets[:, cols.start // 16 : cols.stop // 16]

        nc.vector.tensor_copy(out=xw_g[:], in_=xw[:].indirect(offs_sb[:]))
        w2s_d = deal_scales("w2s_d", w2s, on="xw")
        for cols in halves:
            nc.vector.tensor_copy(out=xs_g[:, cols], in_=xs[:].indirect(entries(offs_sb, cols)))
        w1w_d = deal_words("w1w_d", w1w)
        w1s_d = deal_scales("w1s_d", w1s)

        half_unit = sb("half_unit", [P, PACK], F32)
        neg_unit = sb("neg_unit", [P, PACK], F32)
        nc.vector.tensor_scalar(half_unit[:], unit_sb[:], -0.5, None, ALU.mult)
        nc.vector.tensor_scalar(neg_unit[:], unit_sb[:], -1.0, None, ALU.mult)

        def product(bank, words, scales, t, cols):
            nc.tensor.matmul_mx(
                out=bank[:, cols],
                lhsT=words[:, 2 * P * t : 2 * P * (t + 1)].bitcast(FP4X4),
                lhsT_scale=scales[:, P * t : P * (t + 1)],
                rhs=xw_g[:, cols].bitcast(FP8X4),
                rhs_scale=xs_g[:, cols],
                start=True,
                stop=True,
            )

        te = [psum.tile([P, S], F32, name="te%d" % t, tag="te%d" % t) for t in range(PACK)]
        ne = [psum.tile([P, S], F32, name="ne%d" % t, tag="ne%d" % t) for t in range(PACK)]
        sig_t, sig_d = planes("sig_t"), planes("sig_d")

        def rows(name, on=None):
            return sb(name, [P, PACK, S], F32, on)

        soft_d, neg_temp, cond = rows("soft_d"), rows("neg_temp"), rows("cond")
        neg_press = planes("neg_press")
        for cols in halves:
            for t in range(PACK):
                product(te[t], w2w_d, w2s_d, t, cols)
                nc.scalar.activation(sig_t[t][:, cols], te[t][:, cols], ACT.Sigmoid, scale=-1.0)
        neg_line = rows("neg_line", on="w1s")
        for t in range(PACK):
            nc.vector.tensor_scalar(neg_line[:, t, :], te[t][:], -1.0, -0.2, ALU.mult, ALU.add)
        for t in range(PACK):
            product(ne[t], w1w_d, w1s_d, t, slice(0, S))
            nc.scalar.activation(sig_d[t][:], ne[t][:], ACT.Sigmoid, scale=-1.0)
        log_t, log_d = rows("log_t", on="w1w_d"), rows("log_d")
        for t in range(PACK):
            nc.scalar.activation(log_t[:, t, :], sig_t[t][:], ACT.Ln, scale=math.exp(-0.2), bias=FLOOR)
            nc.scalar.activation(log_d[:, t, :], sig_d[t][:], ACT.Ln, bias=FLOOR)
            nc.vector.tensor_tensor(neg_temp[:, t, :], log_t[:, t, :], neg_line[:, t, :], ALU.min)
            nc.vector.scalar_tensor_tensor(soft_d[:, t, :], log_d[:, t, :], -1.0, ne[t][:], ALU.mult, ALU.max)
        for t in range(PACK):
            nc.vector.scalar_tensor_tensor(neg_press[t][:], soft_d[:, t, :], 0.2, neg_temp[:, t, :], ALU.add, ALU.mult)

        root, sound, outflow = rows("root"), rows("sound"), rows("outflow")
        for pair in (slice(0, 2), slice(2, 4)):
            nc.scalar.activation(root[:, pair, :], neg_temp[:, pair, :], ACT.Sqrt, scale=-1.0)
            nc.scalar.activation(sound[:, pair, :], neg_temp[:, pair, :], ACT.Sqrt, scale=-6.25, bias=0.625)
            for t in range(pair.start, pair.stop):
                nc.vector.scalar_tensor_tensor(
                    cond[:, t, :], neg_temp[:, t, :], half_unit[:, t : t + 1], root[:, t, :], ALU.mult, ALU.mult
                )
            nc.vector.scalar_tensor_tensor(
                outflow[:, pair, :], soft_d[:, pair, :], 0.2, sound[:, pair, :], ALU.add, ALU.mult
            )

        pflux, press_unit = rows("pflux"), rows("press_unit")

        def particles(cols):
            for t in range(PACK):
                nc.vector.tensor_tensor(
                    pflux[:, t, cols], neg_press[t][:].indirect(entries(dn_sb, cols)), outflow[:, t, cols], ALU.add
                )

        cond_up, neg_temp_up = rows("cond_up"), rows("neg_temp_up")
        mag, mag_sq, inv = rows("mag"), rows("mag_sq"), rows("inv")
        slope, cond_sum, hflux = rows("slope"), rows("cond_sum"), rows("hflux")
        carried, limited = rows("carried"), rows("limited")

        def fetch_up(cols):
            for window, fetched in ((neg_temp, neg_temp_up), (cond, cond_up)):
                for t in range(PACK):
                    nc.scalar.activation(fetched[:, t, cols], window[:, t, :].indirect(entries(up_sb, cols)), ACT.Copy)

        def magnitude(cols):
            nc.scalar.activation(mag[:, :, cols], pflux[:, :, cols], ACT.Abs)

        def square(cols):
            nc.scalar.activation(mag_sq[:, :, cols], mag[:, :, cols], ACT.Square, bias=1.25)

        def inverse(cols):
            nc.scalar.activation(inv[:, :, cols], mag_sq[:, :, cols], ACT.Abs_reciprocal_sqrt)

        def neighbours(cols):
            nc.vector.tensor_tensor(slope[:, :, cols], neg_temp[:, :, cols], neg_temp_up[:, :, cols], ALU.subtract)
            nc.vector.tensor_tensor(cond_sum[:, :, cols], cond_up[:, :, cols], cond[:, :, cols], ALU.add)

        def heat(cols):
            nc.vector.tensor_tensor(hflux[:, :, cols], slope[:, :, cols], cond_sum[:, :, cols], ALU.mult)

        def carry(cols):
            nc.vector.tensor_tensor(carried[:, :, cols], hflux[:, :, cols], pflux[:, :, cols], ALU.mult)

        def limit(cols):
            nc.vector.tensor_tensor(limited[:, :, cols], carried[:, :, cols], inv[:, :, cols], ALU.mult)

        def weave(cols):
            hid = sb("hid%d" % cols.start, [P, cols.stop - cols.start, PACK], BF16)
            nc.vector.tensor_tensor(
                hid[:].rearrange("p (c i) t -> p c t i", i=4),
                limited[:, :, cols].rearrange("p t (c i) -> p c t i", i=4),
                press_unit[:, :, cols].rearrange("p t (c i) -> p c t i", i=4),
                ALU.add,
            )
            return hid

        def diagnose(cols, hid, bank):
            width = cols.stop - cols.start
            codes = sb("codes%d" % bank, [P, width], U32)
            scales = sb("scales%d" % bank, [P, width], U8)
            nc.vector.quantize_mx(
                out=codes[:].bitcast(FP8X4), scales=scales[:], in_=hid[:].rearrange("p c t -> p (c t)")
            )
            acc = psum.tile([P, S], F32, name="acc%d" % bank, tag="te%d" % bank)
            nc.tensor.matmul_mx(
                out=acc[:, :width],
                lhsT=w3w[:].bitcast(FP4X4),
                lhsT_scale=w3s[:],
                rhs=codes[:].bitcast(FP8X4),
                rhs_scale=scales[:],
                start=True,
                stop=True,
            )
            result = sb("result%d" % bank, [P, width], F32)
            nc.scalar.copy(out=result[:], in_=acc[:, :width])
            nc.scalar.dma_start(out=out[:, cols], in_=result[:])

        first, second = halves
        quarters = [slice(HALF, HALF + P), slice(HALF + P, S)]
        particles(first)
        for t in range(2):
            nc.vector.tensor_scalar(press_unit[:, t, :], neg_press[t][:], neg_unit[:, t : t + 1], None, ALU.mult)
        fetch_up(first)
        magnitude(first)
        square(first)
        inverse(first)
        for t in range(2, PACK):
            nc.scalar.activation(press_unit[:, t, :], neg_press[t][:], ACT.Copy, scale=neg_unit[:, t : t + 1])
        neighbours(first)
        heat(first)
        carry(first)
        limit(first)
        hid_first = weave(first)
        particles(second)
        fetch_up(second)
        for step in (magnitude, square, inverse):
            for cols in quarters:
                step(cols)
        neighbours(second)
        diagnose(first, hid_first, 0)
        for step in (heat, carry, limit):
            for cols in quarters:
                step(cols)
        hids = [weave(cols) for cols in quarters]
        for bank, cols in enumerate(quarters):
            diagnose(cols, hids[bank], 1 + bank)
